import numpy as np
import ml_dtypes


def mxq(x, axis, fmt="e4m3"):
    dtype, down = {"e4m3": (ml_dtypes.float8_e4m3fn, 7), "e5m2": (ml_dtypes.float8_e5m2, 14)}[fmt]
    v = np.moveaxis(np.asarray(x, np.float32).astype(ml_dtypes.bfloat16).astype(np.float64), axis, -1)
    blocks = v.reshape(v.shape[:-1] + (-1, 32))
    amax = np.abs(blocks).max(-1, keepdims=True)
    byte = np.maximum(np.where(amax > 0, np.frexp(amax)[1] - 1 + 127, 0) - down, 1)
    scale = np.exp2(byte - 127.0)
    codes = (blocks / scale).astype(np.float32).astype(dtype).astype(np.float64)
    return np.moveaxis((codes * scale).reshape(v.shape), -1, axis)


WIDE = False


def mx_kscale(k):
    if not WIDE:
        return np.ones(k)
    levels = np.array([30, -30])
    if k % 512:
        return np.exp2(np.random.permutation(np.resize(levels, k // 32))).repeat(32)
    a = np.empty((k // 512, 16))
    for p in range(k // 512):
        a[p, :8] = np.random.permutation(np.resize(levels, 8))
        for g in range(8):
            far = levels[np.abs(levels - a[p, g]) >= 10]
            a[p, g + 8] = far[np.random.randint(len(far))]
    return np.exp2(a.ravel()).repeat(32)


def f64(x):
    return np.asarray(x).astype(np.float64)


def striped(idx):
    return np.tile(np.asarray(idx).reshape(-1, 16).T, (8, 1)).astype(np.uint16)


def unstriped(offs):
    return offs[:16].T.reshape(-1).astype(np.int64)


E2M1 = np.array([0.0, 0.5, 1.0, 1.5, 2.0, 3.0, 4.0, 6.0, -0.0, -0.5, -1.0, -1.5, -2.0, -3.0, -4.0, -6.0])


def pack_weight(w, fmt):
    k, n = w.shape
    w = f64(np.asarray(w, np.float32).astype(ml_dtypes.bfloat16)).reshape(k // 32, 32, n)
    amax = np.abs(w).max(1)
    if fmt in ("e4m3", "e5m2"):
        byte = np.frexp(amax)[1] - 1 + 127 - (7 if fmt == "e4m3" else 14)
    else:
        mant, ex = np.frexp(amax / 6.0)
        byte = np.where(mant > 0.5, ex, ex - 1) + 127
    byte = np.clip(np.where(amax > 0, byte, 1), 1, 254)
    scaled = (w * np.exp2(127.0 - byte)[:, None, :]).reshape(k, n).astype(np.float32)
    by_word = np.ascontiguousarray(scaled.reshape(k // 512, 128, 4, n).transpose(0, 1, 3, 2))
    if fmt in ("e4m3", "e5m2"):
        words = by_word.astype(ml_dtypes.float8_e4m3fn if fmt == "e4m3" else ml_dtypes.float8_e5m2).view(np.uint8)
    else:
        c = by_word.astype(ml_dtypes.float4_e2m1fn).view(np.uint8) & 0xF
        words = (c[..., 0::2] | (c[..., 1::2] << 4)).reshape(k // 512, 128, 2 * n)
    return np.ascontiguousarray(words), np.ascontiguousarray(byte.astype(np.uint8).reshape(k // 512, 16, n))


def unpack_weight(words, scales, fmt):
    g, _, n = scales.shape
    words = np.ascontiguousarray(words).reshape(g, 128, n, -1)
    if fmt in ("e4m3", "e5m2"):
        vals = words.view(ml_dtypes.float8_e4m3fn if fmt == "e4m3" else ml_dtypes.float8_e5m2).astype(np.float64)
    else:
        nib = np.empty((g, 128, n, 4), np.uint8)
        nib[..., 0::2] = words & 0xF
        nib[..., 1::2] = words >> 4
        vals = E2M1[nib]
    vals = vals * np.repeat(np.exp2(scales.astype(np.float64) - 127.0), 8, axis=1)[..., None]
    return vals.transpose(0, 1, 3, 2).reshape(g * 512, n)


def e4m3fn_bytes(y):
    return np.clip(np.asarray(y, np.float64), -448.0, 448.0).astype(np.float32).astype(ml_dtypes.float8_e4m3fn).view(np.uint8)


def e4m3fn_values(b):
    return np.asarray(b, np.uint8).view(ml_dtypes.float8_e4m3fn).astype(np.float64)


K, T, J, R, V, O, N = 512, 1024, 256, 512, 512, 256, 256


def setup_inputs():
    n = np.random.standard_normal
    idx = np.random.permutation(T)[:J]
    idx2 = np.random.permutation(J)[:O]
    idx3 = np.random.permutation(V)[:O]
    fk = mx_kscale(K)
    fr = mx_kscale(R)
    xtp = pack_weight(n((K, T)) / fk[:, None], "e5m2")
    wp = pack_weight(n((K, R)) * 1 / np.sqrt(K) * fk[:, None] * fr, "e2m1")
    wbp = pack_weight(n((R, N)) * 1 / np.sqrt(R) / fr[:, None], "e2m1")
    return {
        "xt_words": xtp[0],
        "xt_scales": xtp[1],
        "w_words": wp[0],
        "w_scales": wp[1],
        "ca": e4m3fn_bytes(60.0 * n((R, V))),
        "ts": np.tile(np.random.uniform(0.004, 0.02, (1, V)), (128, 1)).astype(np.float32),
        "wb_words": wbp[0],
        "wb_scales": wbp[1],
        "offs": striped(idx),
        "offs2": striped(idx2),
        "offs3": striped(idx3),
    }


def reference(xt_words, xt_scales, w_words, w_scales, ca, ts, wb_words, wb_scales, offs, offs2, offs3):
    idx = unstriped(offs)
    idx2 = unstriped(offs2)
    idx3 = unstriped(offs3)
    xtu = unpack_weight(xt_words, xt_scales, "e5m2")
    wu = unpack_weight(w_words, w_scales, "e2m1")
    wbu = unpack_weight(wb_words, wb_scales, "e2m1")
    xtidxg = xtu[:, idx]
    a = wu.T @ xtidxg
    g1 = e4m3fn_values(ca)[:, idx3] * f64(ts)[:1][:, idx3]
    hid = a[:, idx2] * g1
    hidq = mxq(hid, 0, "e4m3")
    p = wbu.T @ hidq
    return p

@@ -1,0 +1,181 @@
+from contextlib import ExitStack
+
+import concourse.mybir as mybir
+
+K, T, J, R, V, O, N = 512, 1024, 256, 512, 512, 256, 256
+FLOPS = 2 * K * R * J + 2 * R * N * O
+
+F32 = mybir.dt.float32
+BF16 = mybir.dt.bfloat16
+I32 = mybir.dt.int32
+U32 = mybir.dt.uint32
+U16 = mybir.dt.uint16
+U8 = mybir.dt.uint8
+FP8 = mybir.dt.float8_e4m3fn
+E4M3X4 = mybir.dt.float8_e4m3fn_x4
+E5M2X4 = mybir.dt.float8_e5m2_x4
+E2M1X4 = mybir.dt.float4_e2m1fn_x4
+MULT = mybir.AluOpType.mult
+COPY = mybir.ActivationFunctionType.Copy
+
+P = 128
+PACK = 4
+QUADS = 4
+HALVES = 2
+HALF = O // HALVES
+LIST_COLS = HALF // 16
+
+
+def tile_list_ownsteps_kernel(tc, xt_words, xt_scales, w_words, w_scales, ca, ts, wb_words, wb_scales,
+                                 offs, offs2, offs3, out):
+    nc = tc.nc
+    with ExitStack() as ctx:
+        sb = ctx.enter_context(tc.tile_pool(name="sb", bufs=1))
+        ps = ctx.enter_context(tc.psum_pool(name="ps", bufs=1))
+
+        def sbuf(name, shape, dtype):
+            return sb.tile(shape, dtype, name=name, align_bytes=64)
+
+        list1 = sbuf("list1", [P, J // 16], U16)
+        list2 = sbuf("list2", [P, O // 16], U16)
+        list3 = sbuf("list3", [P, O // 16], U16)
+        x_tab = sbuf("x_tab", [P, T], I32)
+        x_tab_sc = sbuf("x_tab_sc", [P, T], U8)
+        w_raw = sbuf("w_raw", [P, 2 * R], U8)
+        w_sc_rows = sbuf("w_sc_rows", [4, QUADS, R // 4], I32)
+        w_sc_raw = sbuf("w_sc_raw", [P, R], U8)
+        wb = sbuf("wb", [P, 2 * N], U8)
+        wb_sc = sbuf("wb_sc", [P, N], U8)
+        ca_rows = [sbuf("ca_rows%d" % t, [P, V], U8) for t in range(PACK)]
+        ts_tab = sbuf("ts_tab", [P, V], F32)
+
+        nc.vector.memset(w_sc_raw[:].bitcast(I32), 0)
+        nc.vector.memset(wb_sc[:].bitcast(I32), 0)
+
+        nc.sync.dma_start(w_sc_rows[:], w_scales[0].bitcast(I32).rearrange("(q r) c -> r q c", r=4))
+        nc.sync.dma_start(list1[:], offs)
+        x_sc_words = xt_scales[0].bitcast(I32)
+        for q in range(QUADS):
+            nc.sync.dma_start(
+                x_tab_sc[32 * q : 32 * q + 32, :].bitcast(I32),
+                x_sc_words[4 * q : 4 * q + 4, :].unsqueeze(0).to_broadcast([8, 4, T // 4]),
+            )
+        nc.sync.dma_start(x_tab[:], xt_words[0].rearrange("p c r -> p (c r)").bitcast(I32))
+        nc.sync.dma_start(w_raw[:].bitcast(I32), w_words[0].bitcast(I32))
+        nc.sync.dma_start(list3[:], offs3)
+        ca_by_slot = ca.rearrange("(p t) v -> p t v", t=PACK)
+        for t in range(PACK):
+            nc.sync.dma_start(ca_rows[t][:], ca_by_slot[:, t, :])
+        nc.sync.dma_start(list2[:], offs2)
+        nc.sync.dma_start(ts_tab[:], ts)
+        nc.sync.dma_start(wb[:].bitcast(I32), wb_words[0].bitcast(I32))
+        wb_sc_words = wb_scales[0].bitcast(I32)
+        for q in range(QUADS):
+            nc.sync.dma_start(wb_sc[32 * q : 32 * q + 4, :].bitcast(I32), wb_sc_words[4 * q : 4 * q + 4, :])
+
+        for q in range(QUADS):
+            nc.vector.tensor_copy(w_sc_raw[32 * q : 32 * q + 4, :].bitcast(I32), w_sc_rows[:, q, :])
+        w_sc = sbuf("w_sc", [P, R], U8)
+        nc.gpsimd.tensor_copy(w_sc[:].rearrange("p (t m) -> p t m", t=PACK),
+                              w_sc_raw[:].rearrange("p (m t) -> p t m", t=PACK))
+        w_dealt = sbuf("w_dealt", [P, 2 * R], U8)
+        nc.scalar.copy(w_dealt[:].bitcast(U16).rearrange("p (t m) -> p t m", t=PACK),
+                       w_raw[:].bitcast(U16).rearrange("p (m t) -> p t m", t=PACK))
+
+        x_sc = sbuf("x_sc", [P, J], U8)
+        nc.vector.tensor_copy(x_sc[:], x_tab_sc[:].indirect(list1[:]))
+        x_picked = sbuf("x_picked", [P, J], U32)
+        nc.vector.tensor_copy(x_picked[:], x_tab[:].bitcast(U32).indirect(list1[:]))
+
+        a_ps = [ps.tile([P, J], F32, name="a_ps%d" % t) for t in range(PACK)]
+        for t in range(PACK):
+            nc.tensor.matmul_mx(
+                a_ps[t][:],
+                lhsT=w_dealt[:, 2 * P * t : 2 * P * (t + 1)].bitcast(E2M1X4),
+                lhsT_scale=w_sc[:, P * t : P * (t + 1)],
+                rhs=x_picked[:].bitcast(E5M2X4),
+                rhs_scale=x_sc[:],
+                start=True,
+                stop=True,
+            )
+
+        a_sb = [sbuf("a_sb%d" % t, [P, J], F32) for t in range(PACK)]
+        a_picked = [sbuf("a_picked%d" % h, [P, PACK, HALF], F32) for h in range(HALVES)]
+        codes = [sbuf("codes%d" % h, [P, PACK, HALF], U8) for h in range(HALVES)]
+        gate = [sbuf("gate%d" % h, [P, PACK, HALF], F32) for h in range(HALVES)]
+        ts_picked = sbuf("ts_picked", [P, O], F32)
+
+        def part(lst, h):
+            return lst[:, LIST_COLS * h : LIST_COLS * (h + 1)]
+
+        def pick_a(h, t):
+            nc.scalar.activation(a_picked[h][:, t, :], a_sb[t][:].indirect(part(list2, h)), COPY)
+
+        def pick_codes(h, t):
+            nc.vector.tensor_copy(codes[h][:, t, :], ca_rows[t][:].indirect(part(list3, h)))
+
+        def make_gate(h):
+            for t in range(PACK):
+                nc.vector.tensor_tensor(
+                    gate[h][:, t, :], codes[h][:, t, :].bitcast(FP8),
+                    ts_picked[:, HALF * h : HALF * (h + 1)], MULT)
+
+        hid = [sbuf("hid%d" % h, [P, PACK * HALF], BF16) for h in range(HALVES)]
+        hid_q = [sbuf("hid_q%d" % h, [P, HALF], U32) for h in range(HALVES)]
+        hid_sc = [sbuf("hid_sc%d" % h, [P, HALF], U8) for h in range(HALVES)]
+
+        def make_hid(h):
+            nc.vector.tensor_tensor(
+                hid[h][:].rearrange("p (c i t) -> p c t i", i=4, t=PACK),
+                a_picked[h][:].rearrange("p t (c i) -> p c t i", i=4),
+                gate[h][:].rearrange("p t (c i) -> p c t i", i=4), MULT)
+
+        def quantise(h):
+            nc.vector.quantize_mx(hid_q[h][:].bitcast(E4M3X4), hid_sc[h][:], hid[h][:])
+
+        def second_product(h, b, acc):
+            nc.tensor.matmul_mx(
+                acc,
+                lhsT=wb[:, 2 * P * b : 2 * P * (b + 1)].bitcast(E2M1X4),
+                lhsT_scale=wb_sc[:, P * b : P * (b + 1)],
+                rhs=hid_q[h][:].bitcast(E4M3X4),
+                rhs_scale=hid_sc[h][:],
+                start=True,
+                stop=True,
+            )
+
+        for t in range(PACK):
+            nc.scalar.activation(a_sb[t][:], a_ps[t][:], COPY)
+            pick_a(0, t)
+            pick_codes(0, t)
+            if t == 0:
+                nc.scalar.activation(ts_picked[:], ts_tab[:].indirect(list3[:]), COPY)
+        pick_codes(1, 0)
+        make_gate(0)
+        for t in range(PACK):
+            pick_a(1, t)
+        pick_codes(1, 1)
+        make_hid(0)
+        pick_codes(1, 2)
+        quantise(0)
+        pick_codes(1, 3)
+
+        out_by_block = out.rearrange("(b p) o -> p b o", p=P)
+        acc0 = ps.tile([P, 2, HALF], F32, name="acc0")
+        res0 = sbuf("res0", [P, 2, HALF], F32)
+        for b in range(2):
+            second_product(0, b, acc0[:, b, :])
+        nc.scalar.copy(res0[:], acc0[:])
+        nc.sync.dma_start(out_by_block[:, :, 0:HALF], res0[:])
+
+        make_gate(1)
+        make_hid(1)
+        quantise(1)
+        acc1 = [ps.tile([P, HALF], F32, name="acc1_%d" % b) for b in range(2)]
+        res1 = [sbuf("res1_%d" % b, [P, HALF], F32) for b in range(2)]
+        for b in range(2):
+            second_product(1, b, acc1[b][:])
+        nc.scalar.copy(res1[0][:], acc1[0][:])
+        nc.scalar.dma_start(out_by_block[:, 0, HALF:O], res1[0][:])
+        nc.vector.tensor_copy(res1[1][:], acc1[1][:])
+        nc.sync.dma_start(out_by_block[:, 1, HALF:O], res1[1][:])

@@ -1,6 +1,7 @@
 from contextlib import ExitStack
 
 import concourse.mybir as mybir
+from concourse.masks import make_identity
 
 K, T, J, R, V, O, N = 512, 1024, 256, 512, 512, 256, 256
 FLOPS = 2 * K * R * J + 2 * R * N * O
@@ -31,6 +32,7 @@ def tile_list_ownsteps_kernel(tc, xt_words, xt_scales, w_words, w_scales, ca, ts
     nc = tc.nc
     with ExitStack() as ctx:
         sb = ctx.enter_context(tc.tile_pool(name="sb", bufs=1))
+        shared = ctx.enter_context(tc.tile_pool(name="shared", bufs=1))
         ps = ctx.enter_context(tc.psum_pool(name="ps", bufs=1))
 
         def sbuf(name, shape, dtype):
@@ -47,32 +49,48 @@ def tile_list_ownsteps_kernel(tc, xt_words, xt_scales, w_words, w_scales, ca, ts
         wb = sbuf("wb", [P, 2 * N], U8)
         wb_sc = sbuf("wb_sc", [P, N], U8)
         ca_rows = [sbuf("ca_rows%d" % t, [P, V], U8) for t in range(PACK)]
-        ts_tab = sbuf("ts_tab", [P, V], F32)
+        ts_tab = shared.tile([P, V], F32, name="ts_tab", offset=6 * J)
+        ts_cols = sbuf("ts_cols", [P, 4], F32)
 
+        x_sc_rows = sbuf("x_sc_rows", [P, 2, T // 4], I32)
         nc.vector.memset(w_sc_raw[:].bitcast(I32), 0)
+        nc.vector.memset(x_tab_sc[64:128, :].bitcast(I32), 0)
         nc.vector.memset(wb_sc[:].bitcast(I32), 0)
 
-        nc.sync.dma_start(w_sc_rows[:], w_scales[0].bitcast(I32).rearrange("(q r) c -> r q c", r=4))
-        nc.sync.dma_start(list1[:], offs)
         x_sc_words = xt_scales[0].bitcast(I32)
-        for q in range(QUADS):
-            nc.sync.dma_start(
+
+        def load_x_scales_filled(q):
+            nc.scalar.dma_start(
                 x_tab_sc[32 * q : 32 * q + 32, :].bitcast(I32),
                 x_sc_words[4 * q : 4 * q + 4, :].unsqueeze(0).to_broadcast([8, 4, T // 4]),
             )
+
+        load_x_scales_filled(0)
+        nc.scalar.dma_start(w_raw[:].bitcast(I32), w_words[0].bitcast(I32))
+        load_x_scales_filled(1)
+        nc.sync.dma_start(x_sc_rows[64:68, :, :], x_sc_words[8:16, :].rearrange("(q r) c -> r q c", r=4))
+        nc.sync.dma_start(ts_cols[:], ts[0].rearrange("(p c) -> p c", c=4))
+        nc.sync.dma_start(w_sc_rows[:], w_scales[0].bitcast(I32).rearrange("(q r) c -> r q c", r=4))
+        nc.sync.dma_start(list1[:], offs)
         nc.sync.dma_start(x_tab[:], xt_words[0].rearrange("p c r -> p (c r)").bitcast(I32))
-        nc.sync.dma_start(w_raw[:].bitcast(I32), w_words[0].bitcast(I32))
         nc.sync.dma_start(list3[:], offs3)
         ca_by_slot = ca.rearrange("(p t) v -> p t v", t=PACK)
         for t in range(PACK):
             nc.sync.dma_start(ca_rows[t][:], ca_by_slot[:, t, :])
         nc.sync.dma_start(list2[:], offs2)
-        nc.sync.dma_start(ts_tab[:], ts)
         nc.sync.dma_start(wb[:].bitcast(I32), wb_words[0].bitcast(I32))
         wb_sc_words = wb_scales[0].bitcast(I32)
         for q in range(QUADS):
             nc.sync.dma_start(wb_sc[32 * q : 32 * q + 4, :].bitcast(I32), wb_sc_words[4 * q : 4 * q + 4, :])
 
+        ident = sbuf("ident", [P, P], F32)
+        make_identity(nc, ident[:])
+        ts_ps = ps.tile([P, 4, P], F32, name="ts_ps")
+        for c in range(4):
+            nc.tensor.transpose(ts_ps[:, c, :], ts_cols[:, c : c + 1].to_broadcast([P, P]), ident[:])
+
+        for q in range(2, QUADS):
+            nc.vector.tensor_copy(x_tab_sc[32 * q : 32 * q + 4, :].bitcast(I32), x_sc_rows[64:68, q - 2, :])
         for q in range(QUADS):
             nc.vector.tensor_copy(w_sc_raw[32 * q : 32 * q + 4, :].bitcast(I32), w_sc_rows[:, q, :])
         w_sc = sbuf("w_sc", [P, R], U8)
@@ -82,100 +100,83 @@ def tile_list_ownsteps_kernel(tc, xt_words, xt_scales, w_words, w_scales, ca, ts
         nc.scalar.copy(w_dealt[:].bitcast(U16).rearrange("p (t m) -> p t m", t=PACK),
                        w_raw[:].bitcast(U16).rearrange("p (m t) -> p t m", t=PACK))
 
+        nc.scalar.activation(ts_tab[:].rearrange("p (m c) -> p m c", c=4), ts_ps[:].rearrange("p c m -> p m c"), COPY)
+
         x_sc = sbuf("x_sc", [P, J], U8)
         nc.vector.tensor_copy(x_sc[:], x_tab_sc[:].indirect(list1[:]))
         x_picked = sbuf("x_picked", [P, J], U32)
-        nc.vector.tensor_copy(x_picked[:], x_tab[:].bitcast(U32).indirect(list1[:]))
+        for g in range(2):
+            nc.vector.tensor_copy(x_picked[:, P * g : P * (g + 1)],
+                                  x_tab[:].bitcast(U32).indirect(list1[:, 8 * g : 8 * (g + 1)]))
 
-        a_ps = [ps.tile([P, J], F32, name="a_ps%d" % t) for t in range(PACK)]
-        for t in range(PACK):
+        a_ps = [ps.tile([P, J], F32, name="a_ps%d" % t, tag="bank%d" % t) for t in range(PACK)]
+        for t, g in ((0, 0), (1, 0), (0, 1), (1, 1), (2, 0), (2, 1), (3, 0), (3, 1)):
             nc.tensor.matmul_mx(
-                a_ps[t][:],
+                a_ps[t][:, P * g : P * (g + 1)],
                 lhsT=w_dealt[:, 2 * P * t : 2 * P * (t + 1)].bitcast(E2M1X4),
                 lhsT_scale=w_sc[:, P * t : P * (t + 1)],
-                rhs=x_picked[:].bitcast(E5M2X4),
-                rhs_scale=x_sc[:],
+                rhs=x_picked[:, P * g : P * (g + 1)].bitcast(E5M2X4),
+                rhs_scale=x_sc[:, P * g : P * (g + 1)],
                 start=True,
                 stop=True,
             )
 
-        a_sb = [sbuf("a_sb%d" % t, [P, J], F32) for t in range(PACK)]
-        a_picked = [sbuf("a_picked%d" % h, [P, PACK, HALF], F32) for h in range(HALVES)]
-        codes = [sbuf("codes%d" % h, [P, PACK, HALF], U8) for h in range(HALVES)]
-        gate = [sbuf("gate%d" % h, [P, PACK, HALF], F32) for h in range(HALVES)]
+        a01 = shared.tile([P, 2 * J], F32, name="a01", offset=0)
+        a2 = shared.tile([P, J], F32, name="a2", offset=12 * J)
+        a3 = shared.tile([P, J], F32, name="a3", offset=8 * J)
+        a_sb = [a01[:, 0:J], a01[:, J : 2 * J], a2[:, 0:J], a3[:]]
+        a_picked = sbuf("a_picked", [P, PACK, O], F32)
+        codes = sbuf("codes", [P, PACK, O], U8)
+        gate = sbuf("gate", [P, PACK, O], F32)
         ts_picked = sbuf("ts_picked", [P, O], F32)
-
-        def part(lst, h):
-            return lst[:, LIST_COLS * h : LIST_COLS * (h + 1)]
-
-        def pick_a(h, t):
-            nc.scalar.activation(a_picked[h][:, t, :], a_sb[t][:].indirect(part(list2, h)), COPY)
-
-        def pick_codes(h, t):
-            nc.vector.tensor_copy(codes[h][:, t, :], ca_rows[t][:].indirect(part(list3, h)))
-
-        def make_gate(h):
-            for t in range(PACK):
-                nc.vector.tensor_tensor(
-                    gate[h][:, t, :], codes[h][:, t, :].bitcast(FP8),
-                    ts_picked[:, HALF * h : HALF * (h + 1)], MULT)
-
         hid = [sbuf("hid%d" % h, [P, PACK * HALF], BF16) for h in range(HALVES)]
         hid_q = [sbuf("hid_q%d" % h, [P, HALF], U32) for h in range(HALVES)]
         hid_sc = [sbuf("hid_sc%d" % h, [P, HALF], U8) for h in range(HALVES)]
 
-        def make_hid(h):
-            nc.vector.tensor_tensor(
-                hid[h][:].rearrange("p (c i t) -> p c t i", i=4, t=PACK),
-                a_picked[h][:].rearrange("p t (c i) -> p c t i", i=4),
-                gate[h][:].rearrange("p t (c i) -> p c t i", i=4), MULT)
+        nc.scalar.activation(ts_picked[:], ts_tab[:].indirect(list3[:]), COPY)
+        for t in range(PACK):
+            nc.scalar.activation(a_sb[t], a_ps[t][:], COPY)
 
-        def quantise(h):
+        def half_of_a(t, h):
+            return (a_picked[:, t, HALF * h : HALF * (h + 1)],
+                    a_sb[t].indirect(list2[:, LIST_COLS * h : LIST_COLS * (h + 1)]))
+
+        nc.scalar.activation(a_picked[:, 0, :], a01[:].indirect(list2[:]), COPY)
+        for t, h in ((1, 0), (2, 0), (3, 0), (1, 1)):
+            nc.scalar.activation(*half_of_a(t, h), COPY)
+        for t in range(PACK):
+            nc.vector.tensor_copy(codes[:, t, :], ca_rows[t][:].indirect(list3[:]))
+        for t in range(PACK):
+            nc.vector.tensor_tensor(gate[:, t, :], codes[:, t, :].bitcast(FP8), ts_picked[:], MULT)
+        for t in (2, 3):
+            nc.vector.tensor_copy(*half_of_a(t, 1))
+        for h in range(HALVES):
+            cols = slice(HALF * h, HALF * (h + 1))
+            nc.vector.tensor_tensor(
+                hid[h][:].rearrange("p (c i t) -> p c t i", i=2, t=PACK),
+                a_picked[:, :, cols].rearrange("p t (c i) -> p c t i", i=2),
+                gate[:, :, cols].rearrange("p t (c i) -> p c t i", i=2), MULT)
+        for h in range(HALVES):
             nc.vector.quantize_mx(hid_q[h][:].bitcast(E4M3X4), hid_sc[h][:], hid[h][:])
 
-        def second_product(h, b, acc):
-            nc.tensor.matmul_mx(
-                acc,
-                lhsT=wb[:, 2 * P * b : 2 * P * (b + 1)].bitcast(E2M1X4),
-                lhsT_scale=wb_sc[:, P * b : P * (b + 1)],
-                rhs=hid_q[h][:].bitcast(E4M3X4),
-                rhs_scale=hid_sc[h][:],
-                start=True,
-                stop=True,
-            )
-
-        for t in range(PACK):
-            nc.scalar.activation(a_sb[t][:], a_ps[t][:], COPY)
-            pick_a(0, t)
-            pick_codes(0, t)
-            if t == 0:
-                nc.scalar.activation(ts_picked[:], ts_tab[:].indirect(list3[:]), COPY)
-        pick_codes(1, 0)
-        make_gate(0)
-        for t in range(PACK):
-            pick_a(1, t)
-        pick_codes(1, 1)
-        make_hid(0)
-        pick_codes(1, 2)
-        quantise(0)
-        pick_codes(1, 3)
-
+        res = [sbuf("res%d" % h, [P, 2, HALF], F32) for h in range(HALVES)]
         out_by_block = out.rearrange("(b p) o -> p b o", p=P)
-        acc0 = ps.tile([P, 2, HALF], F32, name="acc0")
-        res0 = sbuf("res0", [P, 2, HALF], F32)
-        for b in range(2):
-            second_product(0, b, acc0[:, b, :])
-        nc.scalar.copy(res0[:], acc0[:])
-        nc.sync.dma_start(out_by_block[:, :, 0:HALF], res0[:])
-
-        make_gate(1)
-        make_hid(1)
-        quantise(1)
-        acc1 = [ps.tile([P, HALF], F32, name="acc1_%d" % b) for b in range(2)]
-        res1 = [sbuf("res1_%d" % b, [P, HALF], F32) for b in range(2)]
-        for b in range(2):
-            second_product(1, b, acc1[b][:])
-        nc.scalar.copy(res1[0][:], acc1[0][:])
-        nc.scalar.dma_start(out_by_block[:, 0, HALF:O], res1[0][:])
-        nc.vector.tensor_copy(res1[1][:], acc1[1][:])
-        nc.sync.dma_start(out_by_block[:, 1, HALF:O], res1[1][:])
+        for h in range(HALVES):
+            for b in range(2):
+                acc = ps.tile([P, HALF], F32, name="acc%d%d" % (h, b), tag="bank%d" % (2 * h + b))
+                nc.tensor.matmul_mx(
+                    acc[:],
+                    lhsT=wb[:, 2 * P * b : 2 * P * (b + 1)].bitcast(E2M1X4),
+                    lhsT_scale=wb_sc[:, P * b : P * (b + 1)],
+                    rhs=hid_q[h][:].bitcast(E4M3X4),
+                    rhs_scale=hid_sc[h][:],
+                    start=True,
+                    stop=True,
+                )
+                if b == 0:
+                    nc.scalar.copy(res[h][:, b, :], acc[:])
+                else:
+                    nc.vector.tensor_copy(res[h][:, b, :], acc[:])
+        nc.sync.dma_start(out_by_block[:, :, 0:HALF], res[0][:])
+        nc.scalar.dma_start(out_by_block[:, 0, HALF:O], res[1][:, 0, :])
+        nc.sync.dma_start(out_by_block[:, 1, HALF:O], res[1][:, 1, :])

@@ -142,14 +142,17 @@ def tile_list_ownsteps_kernel(tc, xt_words, xt_scales, w_words, w_scales, ca, ts
                     a_sb[t].indirect(list2[:, LIST_COLS * h : LIST_COLS * (h + 1)]))
 
         nc.scalar.activation(a_picked[:, 0, :], a01[:].indirect(list2[:]), COPY)
-        for t, h in ((1, 0), (2, 0), (3, 0), (1, 1)):
+        for t, h in ((1, 0), (2, 0), (1, 1), (2, 1)):
             nc.scalar.activation(*half_of_a(t, h), COPY)
         for t in range(PACK):
             nc.vector.tensor_copy(codes[:, t, :], ca_rows[t][:].indirect(list3[:]))
-        for t in range(PACK):
+        values0 = sbuf("values0", [P, O], F32)
+        nc.gpsimd.tensor_copy(values0[:], codes[:, 0, :].bitcast(FP8))
+        nc.gpsimd.tensor_tensor(gate[:, 0, :], values0[:], ts_picked[:], MULT)
+        for t in range(1, PACK):
             nc.vector.tensor_tensor(gate[:, t, :], codes[:, t, :].bitcast(FP8), ts_picked[:], MULT)
-        for t in (2, 3):
-            nc.vector.tensor_copy(*half_of_a(t, 1))
+        for h in range(HALVES):
+            nc.vector.tensor_copy(*half_of_a(3, h))
         for h in range(HALVES):
             cols = slice(HALF * h, HALF * (h + 1))
             nc.vector.tensor_tensor(

from contextlib import ExitStack

import concourse.mybir as mybir
from concourse.masks import make_identity

K, T, J, R, V, O, N = 512, 1024, 256, 512, 512, 256, 256
FLOPS = 2 * K * R * J + 2 * R * N * O

F32 = mybir.dt.float32
BF16 = mybir.dt.bfloat16
I32 = mybir.dt.int32
U32 = mybir.dt.uint32
U16 = mybir.dt.uint16
U8 = mybir.dt.uint8
FP8 = mybir.dt.float8_e4m3fn
E4M3X4 = mybir.dt.float8_e4m3fn_x4
E5M2X4 = mybir.dt.float8_e5m2_x4
E2M1X4 = mybir.dt.float4_e2m1fn_x4
MULT = mybir.AluOpType.mult
COPY = mybir.ActivationFunctionType.Copy

P = 128
PACK = 4
QUADS = 4
HALVES = 2
HALF = O // HALVES
LIST_COLS = HALF // 16


def tile_list_ownsteps_kernel(tc, xt_words, xt_scales, w_words, w_scales, ca, ts, wb_words, wb_scales,
                                 offs, offs2, offs3, out):
    nc = tc.nc
    with ExitStack() as ctx:
        sb = ctx.enter_context(tc.tile_pool(name="sb", bufs=1))
        shared = ctx.enter_context(tc.tile_pool(name="shared", bufs=1))
        ps = ctx.enter_context(tc.psum_pool(name="ps", bufs=1))

        def sbuf(name, shape, dtype):
            return sb.tile(shape, dtype, name=name, align_bytes=64)

        list1 = sbuf("list1", [P, J // 16], U16)
        list2 = sbuf("list2", [P, O // 16], U16)
        list3 = sbuf("list3", [P, O // 16], U16)
        x_tab = sbuf("x_tab", [P, T], I32)
        x_tab_sc = sbuf("x_tab_sc", [P, T], U8)
        w_raw = sbuf("w_raw", [P, 2 * R], U8)
        w_sc_rows = sbuf("w_sc_rows", [4, QUADS, R // 4], I32)
        w_sc_raw = sbuf("w_sc_raw", [P, R], U8)
        wb = sbuf("wb", [P, 2 * N], U8)
        wb_sc = sbuf("wb_sc", [P, N], U8)
        ca_rows = [sbuf("ca_rows%d" % t, [P, V], U8) for t in range(PACK)]
        ts_tab = shared.tile([P, V], F32, name="ts_tab", offset=6 * J)
        ts_cols = sbuf("ts_cols", [P, 4], F32)

        x_sc_rows = sbuf("x_sc_rows", [P, 2, T // 4], I32)
        nc.vector.memset(w_sc_raw[:].bitcast(I32), 0)
        nc.vector.memset(x_tab_sc[64:128, :].bitcast(I32), 0)
        nc.vector.memset(wb_sc[:].bitcast(I32), 0)

        x_sc_words = xt_scales[0].bitcast(I32)

        def load_x_scales_filled(q):
            nc.scalar.dma_start(
                x_tab_sc[32 * q : 32 * q + 32, :].bitcast(I32),
                x_sc_words[4 * q : 4 * q + 4, :].unsqueeze(0).to_broadcast([8, 4, T // 4]),
            )

        load_x_scales_filled(0)
        nc.scalar.dma_start(w_raw[:].bitcast(I32), w_words[0].bitcast(I32))
        load_x_scales_filled(1)
        nc.sync.dma_start(x_sc_rows[64:68, :, :], x_sc_words[8:16, :].rearrange("(q r) c -> r q c", r=4))
        nc.sync.dma_start(ts_cols[:], ts[0].rearrange("(p c) -> p c", c=4))
        nc.sync.dma_start(w_sc_rows[:], w_scales[0].bitcast(I32).rearrange("(q r) c -> r q c", r=4))
        nc.sync.dma_start(list1[:], offs)
        nc.sync.dma_start(x_tab[:], xt_words[0].rearrange("p c r -> p (c r)").bitcast(I32))
        nc.sync.dma_start(list3[:], offs3)
        ca_by_slot = ca.rearrange("(p t) v -> p t v", t=PACK)
        for t in range(PACK):
            nc.sync.dma_start(ca_rows[t][:], ca_by_slot[:, t, :])
        nc.sync.dma_start(list2[:], offs2)
        nc.sync.dma_start(wb[:].bitcast(I32), wb_words[0].bitcast(I32))
        wb_sc_words = wb_scales[0].bitcast(I32)
        for q in range(QUADS):
            nc.sync.dma_start(wb_sc[32 * q : 32 * q + 4, :].bitcast(I32), wb_sc_words[4 * q : 4 * q + 4, :])

        ident = sbuf("ident", [P, P], F32)
        make_identity(nc, ident[:])
        ts_ps = ps.tile([P, 4, P], F32, name="ts_ps")
        for c in range(4):
            nc.tensor.transpose(ts_ps[:, c, :], ts_cols[:, c : c + 1].to_broadcast([P, P]), ident[:])

        for q in range(2, QUADS):
            nc.vector.tensor_copy(x_tab_sc[32 * q : 32 * q + 4, :].bitcast(I32), x_sc_rows[64:68, q - 2, :])
        for q in range(QUADS):
            nc.vector.tensor_copy(w_sc_raw[32 * q : 32 * q + 4, :].bitcast(I32), w_sc_rows[:, q, :])
        w_sc = sbuf("w_sc", [P, R], U8)
        nc.gpsimd.tensor_copy(w_sc[:].rearrange("p (t m) -> p t m", t=PACK),
                              w_sc_raw[:].rearrange("p (m t) -> p t m", t=PACK))
        w_dealt = sbuf("w_dealt", [P, 2 * R], U8)
        nc.scalar.copy(w_dealt[:].bitcast(U16).rearrange("p (t m) -> p t m", t=PACK),
                       w_raw[:].bitcast(U16).rearrange("p (m t) -> p t m", t=PACK))

        nc.scalar.activation(ts_tab[:].rearrange("p (m c) -> p m c", c=4), ts_ps[:].rearrange("p c m -> p m c"), COPY)

        x_sc = sbuf("x_sc", [P, J], U8)
        nc.vector.tensor_copy(x_sc[:], x_tab_sc[:].indirect(list1[:]))
        x_picked = sbuf("x_picked", [P, J], U32)
        for g in range(2):
            nc.vector.tensor_copy(x_picked[:, P * g : P * (g + 1)],
                                  x_tab[:].bitcast(U32).indirect(list1[:, 8 * g : 8 * (g + 1)]))

        a_ps = [ps.tile([P, J], F32, name="a_ps%d" % t, tag="bank%d" % t) for t in range(PACK)]
        for t, g in ((0, 0), (1, 0), (0, 1), (1, 1), (2, 0), (2, 1), (3, 0), (3, 1)):
            nc.tensor.matmul_mx(
                a_ps[t][:, P * g : P * (g + 1)],
                lhsT=w_dealt[:, 2 * P * t : 2 * P * (t + 1)].bitcast(E2M1X4),
                lhsT_scale=w_sc[:, P * t : P * (t + 1)],
                rhs=x_picked[:, P * g : P * (g + 1)].bitcast(E5M2X4),
                rhs_scale=x_sc[:, P * g : P * (g + 1)],
                start=True,
                stop=True,
            )

        a01 = shared.tile([P, 2 * J], F32, name="a01", offset=0)
        a2 = shared.tile([P, J], F32, name="a2", offset=12 * J)
        a3 = shared.tile([P, J], F32, name="a3", offset=8 * J)
        a_sb = [a01[:, 0:J], a01[:, J : 2 * J], a2[:, 0:J], a3[:]]
        a_picked = sbuf("a_picked", [P, PACK, O], F32)
        codes = sbuf("codes", [P, PACK, O], U8)
        gate = sbuf("gate", [P, PACK, O], F32)
        ts_picked = sbuf("ts_picked", [P, O], F32)
        hid = [sbuf("hid%d" % h, [P, PACK * HALF], BF16) for h in range(HALVES)]
        hid_q = [sbuf("hid_q%d" % h, [P, HALF], U32) for h in range(HALVES)]
        hid_sc = [sbuf("hid_sc%d" % h, [P, HALF], U8) for h in range(HALVES)]

        nc.scalar.activation(ts_picked[:], ts_tab[:].indirect(list3[:]), COPY)
        for t in range(PACK):
            nc.scalar.activation(a_sb[t], a_ps[t][:], COPY)

        def half_of_a(t, h):
            return (a_picked[:, t, HALF * h : HALF * (h + 1)],
                    a_sb[t].indirect(list2[:, LIST_COLS * h : LIST_COLS * (h + 1)]))

        nc.scalar.activation(a_picked[:, 0, :], a01[:].indirect(list2[:]), COPY)
        for t, h in ((1, 0), (2, 0), (1, 1), (2, 1)):
            nc.scalar.activation(*half_of_a(t, h), COPY)
        for t in range(PACK):
            nc.vector.tensor_copy(codes[:, t, :], ca_rows[t][:].indirect(list3[:]))
        values0 = sbuf("values0", [P, O], F32)
        nc.gpsimd.tensor_copy(values0[:], codes[:, 0, :].bitcast(FP8))
        nc.gpsimd.tensor_tensor(gate[:, 0, :], values0[:], ts_picked[:], MULT)
        for t in range(1, PACK):
            nc.vector.tensor_tensor(gate[:, t, :], codes[:, t, :].bitcast(FP8), ts_picked[:], MULT)
        for h in range(HALVES):
            nc.vector.tensor_copy(*half_of_a(3, h))
        for h in range(HALVES):
            cols = slice(HALF * h, HALF * (h + 1))
            nc.vector.tensor_tensor(
                hid[h][:].rearrange("p (c i t) -> p c t i", i=2, t=PACK),
                a_picked[:, :, cols].rearrange("p t (c i) -> p c t i", i=2),
                gate[:, :, cols].rearrange("p t (c i) -> p c t i", i=2), MULT)
        for h in range(HALVES):
            nc.vector.quantize_mx(hid_q[h][:].bitcast(E4M3X4), hid_sc[h][:], hid[h][:])

        res = [sbuf("res%d" % h, [P, 2, HALF], F32) for h in range(HALVES)]
        out_by_block = out.rearrange("(b p) o -> p b o", p=P)
        for h in range(HALVES):
            for b in range(2):
                acc = ps.tile([P, HALF], F32, name="acc%d%d" % (h, b), tag="bank%d" % (2 * h + b))
                nc.tensor.matmul_mx(
                    acc[:],
                    lhsT=wb[:, 2 * P * b : 2 * P * (b + 1)].bitcast(E2M1X4),
                    lhsT_scale=wb_sc[:, P * b : P * (b + 1)],
                    rhs=hid_q[h][:].bitcast(E4M3X4),
                    rhs_scale=hid_sc[h][:],
                    start=True,
                    stop=True,
                )
                if b == 0:
                    nc.scalar.copy(res[h][:, b, :], acc[:])
                else:
                    nc.vector.tensor_copy(res[h][:, b, :], acc[:])
        nc.sync.dma_start(out_by_block[:, :, 0:HALF], res[0][:])
        nc.scalar.dma_start(out_by_block[:, 0, HALF:O], res[1][:, 0, :])
        nc.sync.dma_start(out_by_block[:, 1, HALF:O], res[1][:, 1, :])
